import numpy as np, ml_dtypes
CORES = [56,64,184,192,312,320,440,448]
N = 8
NB, TK, FT = 8, 64, 2
def setup_inputs(rng):
    return {"x": rng.standard_normal((N, NB, 128, TK), dtype=np.float32).astype(ml_dtypes.bfloat16), "w1": (rng.standard_normal((N, 128, FT * 128), dtype=np.float32) / 8).astype(ml_dtypes.bfloat16), "w2": (rng.standard_normal((N, 128, FT * 128), dtype=np.float32) / np.float32(8 * np.sqrt(FT))).astype(ml_dtypes.bfloat16)}
def setup_inputs_big(rng):
    d = setup_inputs(rng)
    for k in ("x",): d[k] = (d[k].astype(np.float32) * 1048576.0).astype(d[k].dtype)
    return d
def setup_inputs_small(rng):
    d = setup_inputs(rng)
    for k in ("x",): d[k] = (d[k].astype(np.float32) * (1 / 1048576.0)).astype(d[k].dtype)
    return d
def reference(x, w1, w2):
    W1, W2 = w1.astype(np.float64), w2.astype(np.float64)
    a = x[0].astype(np.float64)
    for s in range(N):
        a = sum(np.einsum("kf,bkn->bfn", W2[s][:, 128 * f:128 * f + 128], np.maximum(np.einsum("kf,bkn->bfn", W1[s][:, 128 * f:128 * f + 128], a), 0.0)) for f in range(FT))
    y = np.full(x.shape, np.nan, ml_dtypes.bfloat16)
    y[N - 1] = a.astype(ml_dtypes.bfloat16)
    return {"y": y}

@@ -1,0 +1,201 @@
+from concourse.mybir import AluOpType
+
+WORLD = 512
+N, NB, TK, FT = 8, 8, 64, 2
+WC = 2 * FT * 128
+CHUNKS = [("B", 0, 3), ("A", 3, 8)]
+DUP = (2, 3)
+OTHER_DIE = (3, 4, 6)
+K_ON, K_OFF = 8, 8
+
+SCRATCH = {
+    "xs": ("sbuf", [128, NB * TK], "bfloat16"),
+    "act": ("sbuf", [128, NB * TK], "bfloat16"),
+    "yo": ("sbuf", [128, NB * TK], "bfloat16"),
+    "hs": ("sbuf", [128, NB * FT * TK], "bfloat16"),
+    "zero": ("sbuf", [128, FT * TK], "float32"),
+    "wall": ("sbuf", [128, N * WC], "bfloat16"),
+}
+for _m in range(NB):
+    SCRATCH["ps%d" % _m] = ("psum", [128, 512], "float32")
+
+SEMAPHORES = (["ldw1", "ldw2", "zr", "sent", "yarr", "st"] + ["ldx%d" % c for c in range(len(CHUNKS))]
+              + ["aarr%d" % c for c in range(len(CHUNKS))] + ["warr%d" % s for s in range(N)]
+              + ["pe%d" % m for m in range(NB)] + ["ve%d" % m for m in range(NB)])
+
+
+def _same_chip(topo, a, b):
+    return topo.host(a) == topo.host(b) and topo.chip(a) == topo.chip(b)
+
+
+def _links(topo, a, b):
+    if _same_chip(topo, a, b):
+        return 0
+    same_rack = topo.rack(topo.host(a)) == topo.rack(topo.host(b))
+    if topo.mates(a, b) or topo.same_plane(a, b) or (not same_rack and topo.chip(a) == topo.chip(b)):
+        return 1
+    return 2 if same_rack else 3
+
+
+def _mask(topo, src, dst, k):
+    full, m, b = topo.mask(src, dst), 0, 0
+    while k:
+        if (full >> b) & 1:
+            m |= 1 << b
+            k -= 1
+        b += 1
+    return m
+
+
+def _relay(topo, src, dsts, same_die, used):
+    best = None
+    for r in range(WORLD):
+        if r in used or not topo.may_write(src, r) or not all(topo.may_write(r, d) for d in dsts):
+            continue
+        key = (_links(topo, src, r) + _links(topo, r, dsts[0]), _links(topo, src, r),
+               topo.rack(topo.host(r)) != topo.rack(topo.host(dsts[0])), (topo.die(r) == topo.die(src)) != same_die, r)
+        if best is None or key < best:
+            best = key
+    used.add(best[-1])
+    return best[-1]
+
+
+def _plan(T, topo):
+    R = list(T.cores)
+    A = R[-1]
+    two = any(l == "B" for l, _, _ in CHUNKS)
+    B = [c for c in range(WORLD) if c not in R and _same_chip(topo, c, A) and topo.die(c) == topo.die(A)][0] if two else None
+    lane = {"A": A, "B": B}
+    used = set(R) | {A, B}
+    sends, arrive = [], {}
+
+    def add(src, dst, sbuf, dbuf, c0, c1, waits, rsem):
+        k = K_ON if _same_chip(topo, src, dst) else K_OFF
+        sends.append((src, dst, sbuf, dbuf, c0, c1, waits, rsem, k))
+        arrive[(dst, rsem)] = k
+        return [(rsem, k)]
+
+    hop = _relay(topo, R[0], [A], True, used)
+    for c, (l, b0, b1) in enumerate(CHUNKS):
+        w = add(R[0], hop, "act", "xs", b0 * TK, b1 * TK, [("ve%d" % m, 2) for m in range(b0, b1)], "aarr%d" % c)
+        add(hop, lane[l], "xs", "xs", b0 * TK, b1 * TK, w, "aarr%d" % c)
+    loaded = [("ldw1", 16), ("ldw2", 16)]
+    for s in range(1, N - 1):
+        first = B if two else A
+        dsts = [B, A] if (two and s in DUP) else [first]
+        c0, c1, sem = s * WC, (s + 1) * WC, "warr%d" % s
+        frm, w = R[s], loaded
+        if not topo.may_write(frm, first):
+            r = _relay(topo, frm, dsts, s not in OTHER_DIE, used)
+            w = add(frm, r, "wall", "wall", c0, c1, w, sem)
+            frm = r
+        for d in dsts:
+            wd = add(frm, d, "wall", "wall", c0, c1, w, sem)
+            if d == B and len(dsts) == 1:
+                add(B, A, "wall", "wall", c0, c1, wd, sem)
+    nst = N - 1
+    if two:
+        add(A, B, "wall", "wall", (N - 1) * WC, N * WC, loaded, "warr%d" % (N - 1))
+        for l, b0, b1 in CHUNKS:
+            if l == "B":
+                add(B, A, "yo", "yo", b0 * TK, b1 * TK, [("ve%d" % m, 2 * nst) for m in range(b0, b1)], "yarr")
+    return R, lane, sends, arrive
+
+
+def _compute(g, T, chunks, stages, wwait, out_name):
+    te, ve = g.tensor, g.vector
+    ve.memset(T.zero[:], 0.0).then_inc(T.sem.zr, 1)
+    ve.wait_ge(T.sem.zr, 1)
+    seen = set()
+    for blocks, (asem, aval) in chunks:
+        te.wait_ge(T.sem[asem], aval)
+        for i, s in enumerate(stages):
+            src = T.xs if i == 0 else T.act
+            dst = T[out_name] if i == len(stages) - 1 else T.act
+            w0 = s * WC
+            if s not in seen:
+                for sem, val in wwait[s][0]:
+                    te.wait_ge(T.sem[sem], val)
+            for m in blocks:
+                pe, vs, ps = T.sem["pe%d" % m], T.sem["ve%d" % m], T["ps%d" % m]
+                if i:
+                    te.wait_ge(vs, 2 * i)
+                for f in range(FT):
+                    te.matmul(ps[:, f * TK:(f + 1) * TK], T.wall[:, w0 + f * 128:w0 + (f + 1) * 128],
+                              src[:, m * TK:(m + 1) * TK], start=True, stop=True).then_inc(pe, 1)
+                ve.wait_ge(pe, 4 * i + 2)
+                ve.tensor_tensor(out=T.hs[:, m * FT * TK:(m + 1) * FT * TK], in0=ps[:, 0:FT * TK], in1=T.zero[:],
+                                 op=AluOpType.max).then_inc(vs, 1)
+            if s not in seen:
+                for sem, val in wwait[s][1]:
+                    te.wait_ge(T.sem[sem], val)
+                seen.add(s)
+            for m in blocks:
+                pe, vs, ps = T.sem["pe%d" % m], T.sem["ve%d" % m], T["ps%d" % m]
+                te.wait_ge(vs, 2 * i + 1)
+                for f in range(FT):
+                    te.matmul(ps[:, FT * TK:(FT + 1) * TK],
+                              T.wall[:, w0 + (FT + f) * 128:w0 + (FT + f + 1) * 128],
+                              T.hs[:, (m * FT + f) * TK:(m * FT + f + 1) * TK],
+                              start=(f == 0), stop=(f == FT - 1)).then_inc(pe, 1)
+                ve.wait_ge(pe, 4 * i + 4)
+                ve.tensor_copy(out=dst[:, m * TK:(m + 1) * TK], in_=ps[:, FT * TK:(FT + 1) * TK]).then_inc(vs, 1)
+
+
+def rank_program(g, core, T, topo):
+    R, lane, sends, arrive = _plan(T, topo)
+    rank = T.rank_of(core)
+    mine = [s for s in sends if s[0] == core]
+    if rank is None and not mine:
+        return
+    A, B = lane["A"], lane["B"]
+    dq = [g.sync, g.scalar]
+
+    if rank is not None:
+        w0 = rank * WC
+        lw1 = (T.wall[:, w0:w0 + FT * 128], T.w1[:, :], "ldw1")
+        lw2 = (T.wall[:, w0 + FT * 128:w0 + WC], T.w2[:, :], "ldw2")
+        loads = [lw1, lw2]
+        if rank == 0:
+            lx = [(T.xs[:, m * TK:(m + 1) * TK], T.x[m], "ldx%d" % c)
+                  for c, (_, b0, b1) in enumerate(CHUNKS) for m in range(b0, b1)]
+            n0 = CHUNKS[0][2] - CHUNKS[0][1]
+            loads = [lw1] + lx[:n0] + [lw2] + lx[n0:]
+        for j, (o, i_, sem) in enumerate(loads):
+            dq[j % 2].dma_start(o, i_).then_inc(T.sem[sem], 16)
+
+    own = ([("ldw1", 16)], [("ldw2", 16)])
+    if rank == 0:
+        _compute(g, T, [(list(range(b0, b1)), ("ldx%d" % c, 16 * (b1 - b0))) for c, (_, b0, b1) in enumerate(CHUNKS)],
+                 [0], {0: own}, "act")
+    if core == A or core == B:
+        me = "A" if core == A else "B"
+        ww = {s: ([("warr%d" % s, arrive[(core, "warr%d" % s)])], []) if R[s] != core else own for s in range(1, N)}
+        _compute(g, T, [(list(range(b0, b1)), ("aarr%d" % c, arrive[(core, "aarr%d" % c)]))
+                        for c, (l, b0, b1) in enumerate(CHUNKS) if l == me], list(range(1, N)), ww, "yo")
+
+    total = 0
+    for src, dst, sbuf, dbuf, c0, c1, waits, rsem, k in mine:
+        for sem, val in waits:
+            g.wait_ge(T.sem[sem], val)
+        rid, pid = topo.addr(dst, core)
+        g.remote_dma(out_ap=T[dbuf][:, c0:c1], in_ap=T[sbuf][:, c0:c1], remote_sem=T.sem[rsem], local_sem=T.sem.sent,
+                     pid=pid, routing_id=rid, dma_engine_mask=_mask(topo, core, dst, k))
+        total += k
+
+    if core == A:
+        j = 0
+        for l, b0, b1 in CHUNKS:
+            if l == "B":
+                g.scalar.wait_ge(T.sem.yarr, arrive[(A, "yarr")])
+                for m in range(b0, b1):
+                    g.scalar.dma_start(T.y[m], T.yo[:, m * TK:(m + 1) * TK]).then_inc(T.sem.st, 16)
+        own_blocks = [m for l, b0, b1 in CHUNKS if l == "A" for m in range(b0, b1)]
+        for m in own_blocks:
+            q = dq[(len(own_blocks) - 1 - j) % 2]
+            j += 1
+            q.wait_ge(T.sem["ve%d" % m], 2 * (N - 1))
+            q.dma_start(T.y[m], T.yo[:, m * TK:(m + 1) * TK]).then_inc(T.sem.st, 16)
+        g.wait_ge(T.sem.st, 16 * NB)
+    if total:
+        g.wait_ge(T.sem.sent, total)

@@ -1,27 +1,43 @@
-from concourse.mybir import AluOpType
+from concourse.bass import DstId, RemoteDMATransfer
+from concourse.mybir import AluOpType, ActivationFunctionType
 
 WORLD = 512
 N, NB, TK, FT = 8, 8, 64, 2
 WC = 2 * FT * 128
-CHUNKS = [("B", 0, 3), ("A", 3, 8)]
-DUP = (2, 3)
-OTHER_DIE = (3, 4, 6)
-K_ON, K_OFF = 8, 8
+CHUNKS = [("B", 0, 2), ("C", 2, 4), ("D", 4, 5), ("A", 5, 8)]
+MERGED = (3, 4, 5, 6)
+LANE_OPS = []
+for _s in range(1, N):
+    if _s - 1 not in MERGED:
+        LANE_OPS.append(("L1", _s))
+    LANE_OPS.append(("M", _s) if _s in MERGED else ("L2", _s))
+K_ON, K_OFF, K_FWD = 8, 8, 16
+NPAIR = 4
 
 SCRATCH = {
     "xs": ("sbuf", [128, NB * TK], "bfloat16"),
     "act": ("sbuf", [128, NB * TK], "bfloat16"),
     "yo": ("sbuf", [128, NB * TK], "bfloat16"),
-    "hs": ("sbuf", [128, NB * FT * TK], "bfloat16"),
-    "zero": ("sbuf", [128, FT * TK], "float32"),
+    "yd": ("dram", [NB, 128, TK], "bfloat16"),
+    "hs0": ("sbuf", [128, NB * FT * TK], "bfloat16"),
+    "hs1": ("sbuf", [128, NB * FT * TK], "bfloat16"),
+    "zero": ("sbuf", [128, TK], "float32"),
     "wall": ("sbuf", [128, N * WC], "bfloat16"),
+    "cm": ("sbuf", [128, N * WC], "bfloat16"),
+    "ones": ("sbuf", [128, 128], "bfloat16"),
+    "ident": ("sbuf", [128, 128], "bfloat16"),
+    "wt": ("sbuf", [128, FT * 128], "bfloat16"),
 }
-for _m in range(NB):
+for _m in range(2 * NPAIR):
     SCRATCH["ps%d" % _m] = ("psum", [128, 512], "float32")
 
-SEMAPHORES = (["ldw1", "ldw2", "zr", "sent", "yarr", "st"] + ["ldx%d" % c for c in range(len(CHUNKS))]
-              + ["aarr%d" % c for c in range(len(CHUNKS))] + ["warr%d" % s for s in range(N)]
-              + ["pe%d" % m for m in range(NB)] + ["ve%d" % m for m in range(NB)])
+SEMAPHORES = (["ldw1", "ldw2", "zr", "sent", "st", "idn", "t0", "t1", "t2", "t3"]
+              + ["ldx%d" % c for c in range(len(CHUNKS))]
+              + ["aarr%d" % c for c in range(len(CHUNKS))] + ["yarr%d" % c for c in range(len(CHUNKS))]
+              + ["w%d_%d" % (s, h) for s in range(N) for h in range(2)] + ["c%d" % s for s in MERGED]
+              + ["%s%d" % (p, m) for p in ("p0_", "p1_", "p2_", "ve", "se") for m in range(NB)])
+
+_CACHE = {}
 
 
 def _same_chip(topo, a, b):
@@ -61,94 +77,166 @@ def _relay(topo, src, dsts, same_die, used):
 
 
 def _plan(T, topo):
+    if "plan" in _CACHE:
+        return _CACHE["plan"]
     R = list(T.cores)
     A = R[-1]
-    two = any(l == "B" for l, _, _ in CHUNKS)
-    B = [c for c in range(WORLD) if c not in R and _same_chip(topo, c, A) and topo.die(c) == topo.die(A)][0] if two else None
-    lane = {"A": A, "B": B}
-    used = set(R) | {A, B}
+    free = [c for c in range(WORLD) if c not in R and _same_chip(topo, c, A) and topo.die(c) == topo.die(A)]
+    free2 = [c for c in range(WORLD) if c not in R and _same_chip(topo, c, A) and topo.die(c) != topo.die(A)]
+    lane = {"A": A}
+    for l, _, _ in CHUNKS:
+        if l != "A":
+            lane[l] = free[len(lane) - 1]
+    lanes = list(lane.values())
+    helper = {s: free2[j] for j, s in enumerate(MERGED)}
+    used = set(R) | set(lanes) | set(helper.values())
     sends, arrive = [], {}
 
-    def add(src, dst, sbuf, dbuf, c0, c1, waits, rsem):
-        k = K_ON if _same_chip(topo, src, dst) else K_OFF
-        sends.append((src, dst, sbuf, dbuf, c0, c1, waits, rsem, k))
-        arrive[(dst, rsem)] = k
+    def add(src, dsts, sbuf, dbuf, c0, c1, waits, rsem):
+        k = K_FWD if (src in lanes or src in helper.values()) else (K_ON if _same_chip(topo, src, dsts[0]) else K_OFF)
+        sends.append((src, dsts, sbuf, dbuf, c0, c1, waits, rsem, k))
+        for d in dsts:
+            arrive[(d, rsem)] = arrive.get((d, rsem), 0) + k
         return [(rsem, k)]
 
-    hop = _relay(topo, R[0], [A], True, used)
+    hop = _relay(topo, R[0], lanes, True, used)
     for c, (l, b0, b1) in enumerate(CHUNKS):
-        w = add(R[0], hop, "act", "xs", b0 * TK, b1 * TK, [("ve%d" % m, 2) for m in range(b0, b1)], "aarr%d" % c)
-        add(hop, lane[l], "xs", "xs", b0 * TK, b1 * TK, w, "aarr%d" % c)
-    loaded = [("ldw1", 16), ("ldw2", 16)]
-    for s in range(1, N - 1):
-        first = B if two else A
-        dsts = [B, A] if (two and s in DUP) else [first]
-        c0, c1, sem = s * WC, (s + 1) * WC, "warr%d" % s
-        frm, w = R[s], loaded
-        if not topo.may_write(frm, first):
-            r = _relay(topo, frm, dsts, s not in OTHER_DIE, used)
-            w = add(frm, r, "wall", "wall", c0, c1, w, sem)
-            frm = r
-        for d in dsts:
-            wd = add(frm, d, "wall", "wall", c0, c1, w, sem)
-            if d == B and len(dsts) == 1:
-                add(B, A, "wall", "wall", c0, c1, wd, sem)
-    nst = N - 1
-    if two:
-        add(A, B, "wall", "wall", (N - 1) * WC, N * WC, loaded, "warr%d" % (N - 1))
-        for l, b0, b1 in CHUNKS:
-            if l == "B":
-                add(B, A, "yo", "yo", b0 * TK, b1 * TK, [("ve%d" % m, 2 * nst) for m in range(b0, b1)], "yarr")
-    return R, lane, sends, arrive
+        w = add(R[0], [hop], "act", "xs", b0 * TK, b1 * TK, [("ve%d" % m, 2) for m in range(b0, b1)], "aarr%d" % c)
+        add(hop, [lane[l]], "xs", "xs", b0 * TK, b1 * TK, w, "aarr%d" % c)
+    order = [lane[l] for l, _, _ in CHUNKS]
+    j = 0
+    for s in [N - 1] + list(range(1, N - 1)):
+        for h in range(2):
+            c0, sem = s * WC + h * FT * 128, "w%d_%d" % (s, h)
+            c1 = c0 + FT * 128
+            frm, w = R[s], [("ldw%d" % (h + 1), 16)]
+            prod = s if h == 1 else s - 1
+            fan = prod not in MERGED
+            if not fan:
+                target = helper[prod]
+            elif s == N - 1:
+                target = A
+            else:
+                target = order[j % len(order)]
+                j += 1
+            if frm != target:
+                if not topo.may_write(frm, target):
+                    r = _relay(topo, frm, [target], h == 0, used)
+                    w = add(frm, [r], "wall", "wall", c0, c1, w, sem)
+                    frm = r
+                w = add(frm, [target], "wall", "wall", c0, c1, w, sem)
+            if fan:
+                add(target, [d for d in lanes if d != target], "wall", "wall", c0, c1, w, sem)
+    for s in MERGED:
+        add(helper[s], lanes, "cm", "cm", s * WC, (s + 1) * WC, [("t3", FT)], "c%d" % s)
+    for c, (l, b0, b1) in enumerate(CHUNKS):
+        if l != "A":
+            for m in range(b0, b1):
+                add(lane[l], [A], "yo", "yd", m * TK, (m + 1) * TK, [("ve%d" % m, len(LANE_OPS))], "yarr%d" % c)
+    _CACHE["plan"] = (R, lane, helper, sends, arrive)
+    return _CACHE["plan"]
 
 
-def _compute(g, T, chunks, stages, wwait, out_name):
-    te, ve = g.tensor, g.vector
+def _compute(g, T, chunks, ops, wwait, out_name):
+    te, ve, se = g.tensor, g.vector, g.scalar
     ve.memset(T.zero[:], 0.0).then_inc(T.sem.zr, 1)
     ve.wait_ge(T.sem.zr, 1)
-    seen = set()
+    seen, owner, cnt = set(), {}, {}
+    nops = len(ops)
+    HS = [T.hs0, T.hs1]
+
+    def inc(n, m):
+        cnt[(n, m)] = cnt.get((n, m), 0) + 1
+        return T.sem["%s%d" % (n, m)]
+
+    def wait(q, n, m):
+        q.wait_ge(T.sem["%s%d" % (n, m)], cnt[(n, m)])
+
     for blocks, (asem, aval) in chunks:
         te.wait_ge(T.sem[asem], aval)
-        for i, s in enumerate(stages):
-            src = T.xs if i == 0 else T.act
-            dst = T[out_name] if i == len(stages) - 1 else T.act
+        hcur = 0
+        for i, op in enumerate(ops):
+            kind, s = op
             w0 = s * WC
-            if s not in seen:
-                for sem, val in wwait[s][0]:
+            if op not in seen:
+                for sem, val in wwait[op]:
                     te.wait_ge(T.sem[sem], val)
+                seen.add(op)
+            hin, hout = HS[hcur], HS[1 - hcur]
             for m in blocks:
-                pe, vs, ps = T.sem["pe%d" % m], T.sem["ve%d" % m], T["ps%d" % m]
-                if i:
-                    te.wait_ge(vs, 2 * i)
-                for f in range(FT):
-                    te.matmul(ps[:, f * TK:(f + 1) * TK], T.wall[:, w0 + f * 128:w0 + (f + 1) * 128],
-                              src[:, m * TK:(m + 1) * TK], start=True, stop=True).then_inc(pe, 1)
-                ve.wait_ge(pe, 4 * i + 2)
-                ve.tensor_tensor(out=T.hs[:, m * FT * TK:(m + 1) * FT * TK], in0=ps[:, 0:FT * TK], in1=T.zero[:],
-                                 op=AluOpType.max).then_inc(vs, 1)
-            if s not in seen:
-                for sem, val in wwait[s][1]:
-                    te.wait_ge(T.sem[sem], val)
-                seen.add(s)
-            for m in blocks:
-                pe, vs, ps = T.sem["pe%d" % m], T.sem["ve%d" % m], T["ps%d" % m]
-                te.wait_ge(vs, 2 * i + 1)
-                for f in range(FT):
-                    te.matmul(ps[:, FT * TK:(FT + 1) * TK],
-                              T.wall[:, w0 + (FT + f) * 128:w0 + (FT + f + 1) * 128],
-                              T.hs[:, (m * FT + f) * TK:(m * FT + f + 1) * TK],
-                              start=(f == 0), stop=(f == FT - 1)).then_inc(pe, 1)
-                ve.wait_ge(pe, 4 * i + 4)
-                ve.tensor_copy(out=dst[:, m * TK:(m + 1) * TK], in_=ps[:, FT * TK:(FT + 1) * TK]).then_inc(vs, 1)
+                pa, pb = T["ps%d" % (2 * (m % NPAIR))], T["ps%d" % (2 * (m % NPAIR) + 1)]
+                h0, h1, h2 = (m * FT) * TK, (m * FT + 1) * TK, (m * FT + 2) * TK
+                if kind == "L1":
+                    if i:
+                        wait(te, "ve", m)
+                    else:
+                        if m % NPAIR in owner:
+                            te.wait_ge(T.sem["ve%d" % owner[m % NPAIR]], nops)
+                        owner[m % NPAIR] = m
+                    a = (T.act if i else T.xs)[:, m * TK:(m + 1) * TK]
+                    te.matmul(pa[:, 0:TK], T.wall[:, w0:w0 + 128], a, start=True, stop=True).then_inc(inc("p0_", m), 1)
+                    te.matmul(pb[:, 0:TK], T.wall[:, w0 + 128:w0 + 256], a, start=True, stop=True).then_inc(inc("p1_", m), 1)
+                elif kind == "M":
+                    wait(te, "ve", m)
+                    wait(te, "se", m)
+                    for fo, (bank, pn) in enumerate(((pa, "p0_"), (pb, "p1_"))):
+                        for f in range(FT):
+                            te.matmul(bank[:, 0:TK], T.cm[:, w0 + f * 256 + fo * 128:w0 + f * 256 + (fo + 1) * 128],
+                                      hin[:, (m * FT + f) * TK:(m * FT + f + 1) * TK],
+                                      start=(f == 0), stop=(f == FT - 1)).then_inc(inc(pn, m), 1)
+                if kind != "L2":
+                    wait(ve, "p0_", m)
+                    ve.tensor_tensor(out=hout[:, h0:h1], in0=pa[:, 0:TK], in1=T.zero[:],
+                                     op=AluOpType.max).then_inc(inc("ve", m), 1)
+                    wait(se, "p1_", m)
+                    se.activation(hout[:, h1:h2], pb[:, 0:TK], ActivationFunctionType.Relu).then_inc(inc("se", m), 1)
+                else:
+                    dst = T[out_name] if i == nops - 1 else T.act
+                    wait(te, "ve", m)
+                    te.matmul(pa[:, TK:2 * TK], T.wall[:, w0 + 256:w0 + 384], hin[:, h0:h1],
+                              start=True, stop=False).then_inc(inc("p2_", m), 1)
+                    wait(te, "se", m)
+                    te.matmul(pa[:, TK:2 * TK], T.wall[:, w0 + 384:w0 + 512], hin[:, h1:h2],
+                              start=False, stop=True).then_inc(inc("p2_", m), 1)
+                    wait(ve, "p2_", m)
+                    ve.tensor_copy(out=dst[:, m * TK:(m + 1) * TK], in_=pa[:, TK:2 * TK]).then_inc(inc("ve", m), 1)
+            if kind != "L2":
+                hcur = 1 - hcur
+
+
+def _helper(g, T, s, core, arrive):
+    te, ve = g.tensor, g.vector
+    ve.memset(T.ones[:], 1.0).then_inc(T.sem.zr, 1)
+    g.wait_ge(T.sem.zr, 1)
+    g.affine_select(out=T.ident[:], in_=T.ones[:], pattern=[[-1, 128]], compare_op=AluOpType.is_equal, fill=0.0,
+                    base=0, channel_multiplier=1).then_inc(T.sem.idn, 1)
+    te.wait_ge(T.sem.idn, 1)
+    te.wait_ge(T.sem["w%d_1" % s], arrive[(core, "w%d_1" % s)])
+    w0 = s * WC + FT * 128
+    for f in range(FT):
+        te.matmul(T["ps%d" % f][:, 0:128], T.wall[:, w0 + f * 128:w0 + (f + 1) * 128], T.ident[:],
+                  start=True, stop=True).then_inc(T.sem.t0, 1)
+    ve.wait_ge(T.sem.t0, FT)
+    for f in range(FT):
+        ve.tensor_copy(out=T.wt[:, f * 128:(f + 1) * 128], in_=T["ps%d" % f][:, 0:128]).then_inc(T.sem.t1, 1)
+    te.wait_ge(T.sem.t1, FT)
+    te.wait_ge(T.sem["w%d_0" % (s + 1)], arrive[(core, "w%d_0" % (s + 1))])
+    for f in range(FT):
+        te.matmul(T["ps%d" % (FT + f)][:, 0:256], T.wt[:, f * 128:(f + 1) * 128],
+                  T.wall[:, (s + 1) * WC:(s + 1) * WC + 256], start=True, stop=True).then_inc(T.sem.t2, 1)
+    ve.wait_ge(T.sem.t2, FT)
+    for f in range(FT):
+        ve.tensor_copy(out=T.cm[:, s * WC + f * 256:s * WC + (f + 1) * 256],
+                       in_=T["ps%d" % (FT + f)][:, 0:256]).then_inc(T.sem.t3, 1)
 
 
 def rank_program(g, core, T, topo):
-    R, lane, sends, arrive = _plan(T, topo)
+    R, lane, helper, sends, arrive = _plan(T, topo)
     rank = T.rank_of(core)
     mine = [s for s in sends if s[0] == core]
     if rank is None and not mine:
         return
-    A, B = lane["A"], lane["B"]
+    A = lane["A"]
     dq = [g.sync, g.scalar]
 
     if rank is not None:
@@ -164,38 +252,51 @@ def rank_program(g, core, T, topo):
         for j, (o, i_, sem) in enumerate(loads):
             dq[j % 2].dma_start(o, i_).then_inc(T.sem[sem], 16)
 
-    own = ([("ldw1", 16)], [("ldw2", 16)])
     if rank == 0:
         _compute(g, T, [(list(range(b0, b1)), ("ldx%d" % c, 16 * (b1 - b0))) for c, (_, b0, b1) in enumerate(CHUNKS)],
-                 [0], {0: own}, "act")
-    if core == A or core == B:
-        me = "A" if core == A else "B"
-        ww = {s: ([("warr%d" % s, arrive[(core, "warr%d" % s)])], []) if R[s] != core else own for s in range(1, N)}
+                 [("L1", 0), ("L2", 0)], {("L1", 0): [("ldw1", 16)], ("L2", 0): [("ldw2", 16)]}, "act")
+    if core in lane.values():
+        ww = {}
+        for kind, s in LANE_OPS:
+            sem = "c%d" % s if kind == "M" else "w%d_%d" % (s, 0 if kind == "L1" else 1)
+            ww[(kind, s)] = [("ldw1" if kind == "L1" else "ldw2", 16)] if (R[s] == core and kind != "M") \
+                else [(sem, arrive[(core, sem)])]
         _compute(g, T, [(list(range(b0, b1)), ("aarr%d" % c, arrive[(core, "aarr%d" % c)]))
-                        for c, (l, b0, b1) in enumerate(CHUNKS) if l == me], list(range(1, N)), ww, "yo")
+                        for c, (l, b0, b1) in enumerate(CHUNKS) if lane[l] == core], LANE_OPS, ww, "yo")
+    for s in MERGED:
+        if helper[s] == core:
+            _helper(g, T, s, core, arrive)
 
     total = 0
-    for src, dst, sbuf, dbuf, c0, c1, waits, rsem, k in mine:
+    for src, dsts, sbuf, dbuf, c0, c1, waits, rsem, k in mine:
         for sem, val in waits:
             g.wait_ge(T.sem[sem], val)
-        rid, pid = topo.addr(dst, core)
-        g.remote_dma(out_ap=T[dbuf][:, c0:c1], in_ap=T[sbuf][:, c0:c1], remote_sem=T.sem[rsem], local_sem=T.sem.sent,
-                     pid=pid, routing_id=rid, dma_engine_mask=_mask(topo, core, dst, k))
+        ads = [topo.addr(d, core) for d in dsts]
+        out = T.yd[c0 // TK] if dbuf == "yd" else T[dbuf][:, c0:c1]
+        if len(dsts) == 1:
+            g.remote_dma(out_ap=out, in_ap=T[sbuf][:, c0:c1], remote_sem=T.sem[rsem],
+                         local_sem=T.sem.sent, pid=ads[0][1], routing_id=ads[0][0],
+                         dma_engine_mask=_mask(topo, core, dsts[0], k))
+        else:
+            g.remote_dma_fused([RemoteDMATransfer(dst_ids=[DstId(rid=r_, pnc=p_) for r_, p_ in ads],
+                                                  dma_engine_mask=_mask(topo, core, dsts[0], k),
+                                                  remote_sem=T.sem[rsem], srcs=[T[sbuf][:, c0:c1]],
+                                                  dsts=[out for _ in dsts], alu_op=0)],
+                               local_sem=T.sem.sent)
         total += k
 
     if core == A:
-        j = 0
-        for l, b0, b1 in CHUNKS:
-            if l == "B":
-                g.scalar.wait_ge(T.sem.yarr, arrive[(A, "yarr")])
+        nst = 0
+        for c, (l, b0, b1) in enumerate(CHUNKS):
+            if l != "A":
+                g.sync.wait_ge(T.sem["yarr%d" % c], arrive[(A, "yarr%d" % c)])
+                g.sync.dma_start(T.y[b0:b1], T.yd[b0:b1]).then_inc(T.sem.st, 16)
+                nst += 1
+            else:
                 for m in range(b0, b1):
+                    g.scalar.wait_ge(T.sem["ve%d" % m], len(LANE_OPS))
                     g.scalar.dma_start(T.y[m], T.yo[:, m * TK:(m + 1) * TK]).then_inc(T.sem.st, 16)
-        own_blocks = [m for l, b0, b1 in CHUNKS if l == "A" for m in range(b0, b1)]
-        for m in own_blocks:
-            q = dq[(len(own_blocks) - 1 - j) % 2]
-            j += 1
-            q.wait_ge(T.sem["ve%d" % m], 2 * (N - 1))
-            q.dma_start(T.y[m], T.yo[:, m * TK:(m + 1) * TK]).then_inc(T.sem.st, 16)
-        g.wait_ge(T.sem.st, 16 * NB)
+                    nst += 1
+        g.wait_ge(T.sem.st, 16 * nst)
     if total:
         g.wait_ge(T.sem.sent, total)

from concourse.bass import DstId, RemoteDMATransfer
from concourse.mybir import AluOpType, ActivationFunctionType

WORLD = 512
N, NB, TK, FT = 8, 8, 64, 2
WC = 2 * FT * 128
CHUNKS = [("B", 0, 2), ("C", 2, 4), ("D", 4, 5), ("A", 5, 8)]
MERGED = (3, 4, 5, 6)
LANE_OPS = []
for _s in range(1, N):
    if _s - 1 not in MERGED:
        LANE_OPS.append(("L1", _s))
    LANE_OPS.append(("M", _s) if _s in MERGED else ("L2", _s))
K_ON, K_OFF, K_FWD = 8, 8, 16
NPAIR = 4

SCRATCH = {
    "xs": ("sbuf", [128, NB * TK], "bfloat16"),
    "act": ("sbuf", [128, NB * TK], "bfloat16"),
    "yo": ("sbuf", [128, NB * TK], "bfloat16"),
    "yd": ("dram", [NB, 128, TK], "bfloat16"),
    "hs0": ("sbuf", [128, NB * FT * TK], "bfloat16"),
    "hs1": ("sbuf", [128, NB * FT * TK], "bfloat16"),
    "zero": ("sbuf", [128, TK], "float32"),
    "wall": ("sbuf", [128, N * WC], "bfloat16"),
    "cm": ("sbuf", [128, N * WC], "bfloat16"),
    "ones": ("sbuf", [128, 128], "bfloat16"),
    "ident": ("sbuf", [128, 128], "bfloat16"),
    "wt": ("sbuf", [128, FT * 128], "bfloat16"),
}
for _m in range(2 * NPAIR):
    SCRATCH["ps%d" % _m] = ("psum", [128, 512], "float32")

SEMAPHORES = (["ldw1", "ldw2", "zr", "sent", "st", "idn", "t0", "t1", "t2", "t3"]
              + ["ldx%d" % c for c in range(len(CHUNKS))]
              + ["aarr%d" % c for c in range(len(CHUNKS))] + ["yarr%d" % c for c in range(len(CHUNKS))]
              + ["w%d_%d" % (s, h) for s in range(N) for h in range(2)] + ["c%d" % s for s in MERGED]
              + ["%s%d" % (p, m) for p in ("p0_", "p1_", "p2_", "ve", "se") for m in range(NB)])

_CACHE = {}


def _same_chip(topo, a, b):
    return topo.host(a) == topo.host(b) and topo.chip(a) == topo.chip(b)


def _links(topo, a, b):
    if _same_chip(topo, a, b):
        return 0
    same_rack = topo.rack(topo.host(a)) == topo.rack(topo.host(b))
    if topo.mates(a, b) or topo.same_plane(a, b) or (not same_rack and topo.chip(a) == topo.chip(b)):
        return 1
    return 2 if same_rack else 3


def _mask(topo, src, dst, k):
    full, m, b = topo.mask(src, dst), 0, 0
    while k:
        if (full >> b) & 1:
            m |= 1 << b
            k -= 1
        b += 1
    return m


def _relay(topo, src, dsts, same_die, used):
    best = None
    for r in range(WORLD):
        if r in used or not topo.may_write(src, r) or not all(topo.may_write(r, d) for d in dsts):
            continue
        key = (_links(topo, src, r) + _links(topo, r, dsts[0]), _links(topo, src, r),
               topo.rack(topo.host(r)) != topo.rack(topo.host(dsts[0])), (topo.die(r) == topo.die(src)) != same_die, r)
        if best is None or key < best:
            best = key
    used.add(best[-1])
    return best[-1]


def _plan(T, topo):
    if "plan" in _CACHE:
        return _CACHE["plan"]
    R = list(T.cores)
    A = R[-1]
    free = [c for c in range(WORLD) if c not in R and _same_chip(topo, c, A) and topo.die(c) == topo.die(A)]
    free2 = [c for c in range(WORLD) if c not in R and _same_chip(topo, c, A) and topo.die(c) != topo.die(A)]
    lane = {"A": A}
    for l, _, _ in CHUNKS:
        if l != "A":
            lane[l] = free[len(lane) - 1]
    lanes = list(lane.values())
    helper = {s: free2[j] for j, s in enumerate(MERGED)}
    used = set(R) | set(lanes) | set(helper.values())
    sends, arrive = [], {}

    def add(src, dsts, sbuf, dbuf, c0, c1, waits, rsem):
        k = K_FWD if (src in lanes or src in helper.values()) else (K_ON if _same_chip(topo, src, dsts[0]) else K_OFF)
        sends.append((src, dsts, sbuf, dbuf, c0, c1, waits, rsem, k))
        for d in dsts:
            arrive[(d, rsem)] = arrive.get((d, rsem), 0) + k
        return [(rsem, k)]

    hop = _relay(topo, R[0], lanes, True, used)
    for c, (l, b0, b1) in enumerate(CHUNKS):
        w = add(R[0], [hop], "act", "xs", b0 * TK, b1 * TK, [("ve%d" % m, 2) for m in range(b0, b1)], "aarr%d" % c)
        add(hop, [lane[l]], "xs", "xs", b0 * TK, b1 * TK, w, "aarr%d" % c)
    order = [lane[l] for l, _, _ in CHUNKS]
    j = 0
    for s in [N - 1] + list(range(1, N - 1)):
        for h in range(2):
            c0, sem = s * WC + h * FT * 128, "w%d_%d" % (s, h)
            c1 = c0 + FT * 128
            frm, w = R[s], [("ldw%d" % (h + 1), 16)]
            prod = s if h == 1 else s - 1
            fan = prod not in MERGED
            if not fan:
                target = helper[prod]
            elif s == N - 1:
                target = A
            else:
                target = order[j % len(order)]
                j += 1
            if frm != target:
                if not topo.may_write(frm, target):
                    r = _relay(topo, frm, [target], h == 0, used)
                    w = add(frm, [r], "wall", "wall", c0, c1, w, sem)
                    frm = r
                w = add(frm, [target], "wall", "wall", c0, c1, w, sem)
            if fan:
                add(target, [d for d in lanes if d != target], "wall", "wall", c0, c1, w, sem)
    for s in MERGED:
        add(helper[s], lanes, "cm", "cm", s * WC, (s + 1) * WC, [("t3", FT)], "c%d" % s)
    for c, (l, b0, b1) in enumerate(CHUNKS):
        if l != "A":
            for m in range(b0, b1):
                add(lane[l], [A], "yo", "yd", m * TK, (m + 1) * TK, [("ve%d" % m, len(LANE_OPS))], "yarr%d" % c)
    _CACHE["plan"] = (R, lane, helper, sends, arrive)
    return _CACHE["plan"]


def _compute(g, T, chunks, ops, wwait, out_name):
    te, ve, se = g.tensor, g.vector, g.scalar
    ve.memset(T.zero[:], 0.0).then_inc(T.sem.zr, 1)
    ve.wait_ge(T.sem.zr, 1)
    seen, owner, cnt = set(), {}, {}
    nops = len(ops)
    HS = [T.hs0, T.hs1]

    def inc(n, m):
        cnt[(n, m)] = cnt.get((n, m), 0) + 1
        return T.sem["%s%d" % (n, m)]

    def wait(q, n, m):
        q.wait_ge(T.sem["%s%d" % (n, m)], cnt[(n, m)])

    for blocks, (asem, aval) in chunks:
        te.wait_ge(T.sem[asem], aval)
        hcur = 0
        for i, op in enumerate(ops):
            kind, s = op
            w0 = s * WC
            if op not in seen:
                for sem, val in wwait[op]:
                    te.wait_ge(T.sem[sem], val)
                seen.add(op)
            hin, hout = HS[hcur], HS[1 - hcur]
            for m in blocks:
                pa, pb = T["ps%d" % (2 * (m % NPAIR))], T["ps%d" % (2 * (m % NPAIR) + 1)]
                h0, h1, h2 = (m * FT) * TK, (m * FT + 1) * TK, (m * FT + 2) * TK
                if kind == "L1":
                    if i:
                        wait(te, "ve", m)
                    else:
                        if m % NPAIR in owner:
                            te.wait_ge(T.sem["ve%d" % owner[m % NPAIR]], nops)
                        owner[m % NPAIR] = m
                    a = (T.act if i else T.xs)[:, m * TK:(m + 1) * TK]
                    te.matmul(pa[:, 0:TK], T.wall[:, w0:w0 + 128], a, start=True, stop=True).then_inc(inc("p0_", m), 1)
                    te.matmul(pb[:, 0:TK], T.wall[:, w0 + 128:w0 + 256], a, start=True, stop=True).then_inc(inc("p1_", m), 1)
                elif kind == "M":
                    wait(te, "ve", m)
                    wait(te, "se", m)
                    for fo, (bank, pn) in enumerate(((pa, "p0_"), (pb, "p1_"))):
                        for f in range(FT):
                            te.matmul(bank[:, 0:TK], T.cm[:, w0 + f * 256 + fo * 128:w0 + f * 256 + (fo + 1) * 128],
                                      hin[:, (m * FT + f) * TK:(m * FT + f + 1) * TK],
                                      start=(f == 0), stop=(f == FT - 1)).then_inc(inc(pn, m), 1)
                if kind != "L2":
                    wait(ve, "p0_", m)
                    ve.tensor_tensor(out=hout[:, h0:h1], in0=pa[:, 0:TK], in1=T.zero[:],
                                     op=AluOpType.max).then_inc(inc("ve", m), 1)
                    wait(se, "p1_", m)
                    se.activation(hout[:, h1:h2], pb[:, 0:TK], ActivationFunctionType.Relu).then_inc(inc("se", m), 1)
                else:
                    dst = T[out_name] if i == nops - 1 else T.act
                    wait(te, "ve", m)
                    te.matmul(pa[:, TK:2 * TK], T.wall[:, w0 + 256:w0 + 384], hin[:, h0:h1],
                              start=True, stop=False).then_inc(inc("p2_", m), 1)
                    wait(te, "se", m)
                    te.matmul(pa[:, TK:2 * TK], T.wall[:, w0 + 384:w0 + 512], hin[:, h1:h2],
                              start=False, stop=True).then_inc(inc("p2_", m), 1)
                    wait(ve, "p2_", m)
                    ve.tensor_copy(out=dst[:, m * TK:(m + 1) * TK], in_=pa[:, TK:2 * TK]).then_inc(inc("ve", m), 1)
            if kind != "L2":
                hcur = 1 - hcur


def _helper(g, T, s, core, arrive):
    te, ve = g.tensor, g.vector
    ve.memset(T.ones[:], 1.0).then_inc(T.sem.zr, 1)
    g.wait_ge(T.sem.zr, 1)
    g.affine_select(out=T.ident[:], in_=T.ones[:], pattern=[[-1, 128]], compare_op=AluOpType.is_equal, fill=0.0,
                    base=0, channel_multiplier=1).then_inc(T.sem.idn, 1)
    te.wait_ge(T.sem.idn, 1)
    te.wait_ge(T.sem["w%d_1" % s], arrive[(core, "w%d_1" % s)])
    w0 = s * WC + FT * 128
    for f in range(FT):
        te.matmul(T["ps%d" % f][:, 0:128], T.wall[:, w0 + f * 128:w0 + (f + 1) * 128], T.ident[:],
                  start=True, stop=True).then_inc(T.sem.t0, 1)
    ve.wait_ge(T.sem.t0, FT)
    for f in range(FT):
        ve.tensor_copy(out=T.wt[:, f * 128:(f + 1) * 128], in_=T["ps%d" % f][:, 0:128]).then_inc(T.sem.t1, 1)
    te.wait_ge(T.sem.t1, FT)
    te.wait_ge(T.sem["w%d_0" % (s + 1)], arrive[(core, "w%d_0" % (s + 1))])
    for f in range(FT):
        te.matmul(T["ps%d" % (FT + f)][:, 0:256], T.wt[:, f * 128:(f + 1) * 128],
                  T.wall[:, (s + 1) * WC:(s + 1) * WC + 256], start=True, stop=True).then_inc(T.sem.t2, 1)
    ve.wait_ge(T.sem.t2, FT)
    for f in range(FT):
        ve.tensor_copy(out=T.cm[:, s * WC + f * 256:s * WC + (f + 1) * 256],
                       in_=T["ps%d" % (FT + f)][:, 0:256]).then_inc(T.sem.t3, 1)


def rank_program(g, core, T, topo):
    R, lane, helper, sends, arrive = _plan(T, topo)
    rank = T.rank_of(core)
    mine = [s for s in sends if s[0] == core]
    if rank is None and not mine:
        return
    A = lane["A"]
    dq = [g.sync, g.scalar]

    if rank is not None:
        w0 = rank * WC
        lw1 = (T.wall[:, w0:w0 + FT * 128], T.w1[:, :], "ldw1")
        lw2 = (T.wall[:, w0 + FT * 128:w0 + WC], T.w2[:, :], "ldw2")
        loads = [lw1, lw2]
        if rank == 0:
            lx = [(T.xs[:, m * TK:(m + 1) * TK], T.x[m], "ldx%d" % c)
                  for c, (_, b0, b1) in enumerate(CHUNKS) for m in range(b0, b1)]
            n0 = CHUNKS[0][2] - CHUNKS[0][1]
            loads = [lw1] + lx[:n0] + [lw2] + lx[n0:]
        for j, (o, i_, sem) in enumerate(loads):
            dq[j % 2].dma_start(o, i_).then_inc(T.sem[sem], 16)

    if rank == 0:
        _compute(g, T, [(list(range(b0, b1)), ("ldx%d" % c, 16 * (b1 - b0))) for c, (_, b0, b1) in enumerate(CHUNKS)],
                 [("L1", 0), ("L2", 0)], {("L1", 0): [("ldw1", 16)], ("L2", 0): [("ldw2", 16)]}, "act")
    if core in lane.values():
        ww = {}
        for kind, s in LANE_OPS:
            sem = "c%d" % s if kind == "M" else "w%d_%d" % (s, 0 if kind == "L1" else 1)
            ww[(kind, s)] = [("ldw1" if kind == "L1" else "ldw2", 16)] if (R[s] == core and kind != "M") \
                else [(sem, arrive[(core, sem)])]
        _compute(g, T, [(list(range(b0, b1)), ("aarr%d" % c, arrive[(core, "aarr%d" % c)]))
                        for c, (l, b0, b1) in enumerate(CHUNKS) if lane[l] == core], LANE_OPS, ww, "yo")
    for s in MERGED:
        if helper[s] == core:
            _helper(g, T, s, core, arrive)

    total = 0
    for src, dsts, sbuf, dbuf, c0, c1, waits, rsem, k in mine:
        for sem, val in waits:
            g.wait_ge(T.sem[sem], val)
        ads = [topo.addr(d, core) for d in dsts]
        out = T.yd[c0 // TK] if dbuf == "yd" else T[dbuf][:, c0:c1]
        if len(dsts) == 1:
            g.remote_dma(out_ap=out, in_ap=T[sbuf][:, c0:c1], remote_sem=T.sem[rsem],
                         local_sem=T.sem.sent, pid=ads[0][1], routing_id=ads[0][0],
                         dma_engine_mask=_mask(topo, core, dsts[0], k))
        else:
            g.remote_dma_fused([RemoteDMATransfer(dst_ids=[DstId(rid=r_, pnc=p_) for r_, p_ in ads],
                                                  dma_engine_mask=_mask(topo, core, dsts[0], k),
                                                  remote_sem=T.sem[rsem], srcs=[T[sbuf][:, c0:c1]],
                                                  dsts=[out for _ in dsts], alu_op=0)],
                               local_sem=T.sem.sent)
        total += k

    if core == A:
        nst = 0
        for c, (l, b0, b1) in enumerate(CHUNKS):
            if l != "A":
                g.sync.wait_ge(T.sem["yarr%d" % c], arrive[(A, "yarr%d" % c)])
                g.sync.dma_start(T.y[b0:b1], T.yd[b0:b1]).then_inc(T.sem.st, 16)
                nst += 1
            else:
                for m in range(b0, b1):
                    g.scalar.wait_ge(T.sem["ve%d" % m], len(LANE_OPS))
                    g.scalar.dma_start(T.y[m], T.yo[:, m * TK:(m + 1) * TK]).then_inc(T.sem.st, 16)
                    nst += 1
        g.wait_ge(T.sem.st, 16 * nst)
    if total:
        g.wait_ge(T.sem.sent, total)
